import numpy as np
import ml_dtypes


def mxq(x, axis, fmt="e4m3"):
    dtype, down = {"e4m3": (ml_dtypes.float8_e4m3fn, 7), "e5m2": (ml_dtypes.float8_e5m2, 14)}[fmt]
    v = np.moveaxis(np.asarray(x, np.float32).astype(ml_dtypes.bfloat16).astype(np.float64), axis, -1)
    blocks = v.reshape(v.shape[:-1] + (-1, 32))
    amax = np.abs(blocks).max(-1, keepdims=True)
    byte = np.maximum(np.where(amax > 0, np.frexp(amax)[1] - 1 + 127, 0) - down, 1)
    scale = np.exp2(byte - 127.0)
    codes = (blocks / scale).astype(np.float32).astype(dtype).astype(np.float64)
    return np.moveaxis((codes * scale).reshape(v.shape), -1, axis)


WIDE = False


def mx_kscale(k):
    if not WIDE:
        return np.ones(k)
    levels = np.array([10, -10, 5, -5, 0])
    if k % 512:
        return np.exp2(np.random.permutation(np.resize(levels, k // 32))).repeat(32)
    a = np.empty((k // 512, 16))
    for p in range(k // 512):
        a[p, :8] = np.random.permutation(np.resize(levels, 8))
        for g in range(8):
            far = levels[np.abs(levels - a[p, g]) >= 10]
            a[p, g + 8] = far[np.random.randint(len(far))]
    return np.exp2(a.ravel()).repeat(32)


def f64(x):
    return np.asarray(x).astype(np.float64)


def striped8(idx):
    return np.asarray(idx).reshape(8, -1, 16).transpose(0, 2, 1).reshape(128, -1).astype(np.uint16)


def unstriped8(offs):
    return offs.reshape(8, 16, -1).transpose(0, 2, 1).reshape(8, -1).astype(np.int64)


def pick8(x, idx, run):
    r = np.arange(len(x))
    return x[r[:, None], idx[r % (8 * run) // run]]


E2M1 = np.array([0.0, 0.5, 1.0, 1.5, 2.0, 3.0, 4.0, 6.0, -0.0, -0.5, -1.0, -1.5, -2.0, -3.0, -4.0, -6.0])


def pack_weight(w, fmt):
    k, n = w.shape
    w = f64(np.asarray(w, np.float32).astype(ml_dtypes.bfloat16)).reshape(k // 32, 32, n)
    amax = np.abs(w).max(1)
    if fmt == "e4m3":
        byte = np.frexp(amax)[1] - 1 + 127 - 7
    else:
        mant, ex = np.frexp(amax / 6.0)
        byte = np.where(mant > 0.5, ex, ex - 1) + 127
    byte = np.clip(np.where(amax > 0, byte, 1), 1, 254)
    scaled = (w * np.exp2(127.0 - byte)[:, None, :]).reshape(k, n).astype(np.float32)
    by_word = np.ascontiguousarray(scaled.reshape(k // 512, 128, 4, n).transpose(0, 1, 3, 2))
    if fmt == "e4m3":
        words = by_word.astype(ml_dtypes.float8_e4m3fn).view(np.uint8)
    else:
        c = by_word.astype(ml_dtypes.float4_e2m1fn).view(np.uint8) & 0xF
        words = (c[..., 0::2] | (c[..., 1::2] << 4)).reshape(k // 512, 128, 2 * n)
    return np.ascontiguousarray(words), np.ascontiguousarray(byte.astype(np.uint8).reshape(k // 512, 16, n))


def unpack_weight(words, scales, fmt):
    g, _, n = scales.shape
    words = np.ascontiguousarray(words).reshape(g, 128, n, -1)
    if fmt == "e4m3":
        vals = words.view(ml_dtypes.float8_e4m3fn).astype(np.float64)
    else:
        nib = np.empty((g, 128, n, 4), np.uint8)
        nib[..., 0::2] = words & 0xF
        nib[..., 1::2] = words >> 4
        vals = E2M1[nib]
    vals = vals * np.repeat(np.exp2(scales.astype(np.float64) - 127.0), 8, axis=1)[..., None]
    return vals.transpose(0, 1, 3, 2).reshape(g * 512, n)


def sgn(shape):
    return np.random.uniform(0.5, 2.0, shape) * np.where(np.random.standard_normal(shape) < 0, -1.0, 1.0)


D, T, U, I, Q = 512, 1024, 1024, 512, 128


def setup_inputs():
    n = np.random.standard_normal
    idx = np.stack([np.random.permutation(T)[:I] for _ in range(8)])
    idx2 = np.stack([np.random.permutation(U)[:I] for _ in range(8)])
    idx3 = np.stack([np.random.permutation(T)[:I] for _ in range(8)])
    idx4 = np.stack([np.random.permutation(U)[:I] for _ in range(8)])
    idx5 = np.stack([np.random.permutation(T)[:I] for _ in range(8)])
    fd = mx_kscale(D)
    cachep = pack_weight(n((D, T)) / fd[:, None], "e4m3")
    draftp = pack_weight(n((D, U)) / fd[:, None], "e2m1")
    return {
        "query": (n((D, Q)) * 1.0 / np.sqrt(D) * fd[:, None]).astype(np.float32),
        "cache_words": cachep[0],
        "cache_scales": cachep[1],
        "draft_words": draftp[0],
        "draft_scales": draftp[1],
        "sa": (sgn((Q, 1))).astype(np.float32),
        "offs": striped8(idx),
        "offs2": striped8(idx2),
        "offs3": striped8(idx3),
        "offs4": striped8(idx4),
        "offs5": striped8(idx5),
    }


def reference(query, cache_words, cache_scales, draft_words, draft_scales, sa, offs, offs2, offs3, offs4, offs5):
    idx = unstriped8(offs)
    idx2 = unstriped8(offs2)
    idx3 = unstriped8(offs3)
    idx4 = unstriped8(offs4)
    idx5 = unstriped8(offs5)
    cacheu = unpack_weight(cache_words, cache_scales, "e4m3")
    draftu = unpack_weight(draft_words, draft_scales, "e2m1")
    queryq = mxq(f64(query), 0, "e4m3")
    a = queryq.T @ cacheu
    b = queryq.T @ draftu
    w = pick8(a, idx, 16) * f64(sa)
    v = np.square(w) * 0.5
    f1 = np.zeros((Q, U))
    f1[np.arange(Q)[:, None], idx2[np.arange(Q) % 128 // 16]] = v
    bb = b - f1
    r = np.maximum(pick8(bb, idx4, 16), w)
    f2 = np.zeros((Q, T))
    f2[np.arange(Q)[:, None], idx3[np.arange(Q) % 128 // 16]] = r
    aa = a + f2
    y = np.minimum(pick8(aa, idx5, 16), pick8(b, idx4, 16))
    return y

@@ -1,0 +1,147 @@
+from contextlib import ExitStack
+
+import concourse.mybir as mybir
+
+D, T, U, I, Q = 512, 1024, 1024, 512, 128
+FLOPS = 2 * D * Q * (T + U)
+
+F32 = mybir.dt.float32
+BF16 = mybir.dt.bfloat16
+I32 = mybir.dt.int32
+U32 = mybir.dt.uint32
+U16 = mybir.dt.uint16
+U8 = mybir.dt.uint8
+FP8X4 = mybir.dt.float8_e4m3fn_x4
+FP4X4 = mybir.dt.float4_e2m1fn_x4
+COPY = mybir.ActivationFunctionType.Copy
+ALU = mybir.AluOpType
+
+P = 128
+PACK = 4
+HALF = I // 2
+
+
+def tile_attend_squaresout_two_kernel(tc, query, cache_words, cache_scales, draft_words, draft_scales, sa,
+                                       offs, offs2, offs3, offs4, offs5, out):
+    nc = tc.nc
+    with ExitStack() as ctx:
+        sb = ctx.enter_context(tc.tile_pool(name="sb", bufs=1))
+        ps = ctx.enter_context(tc.psum_pool(name="ps", bufs=1))
+
+        def list_tile(name):
+            return sb.tile([P, I // 16], U16, name=name)
+
+        def entries(lst, lo, hi):
+            return lst[:, lo // 16 : hi // 16]
+
+        def load_scale_rows(queue, plane, rows):
+            for quad in range(4):
+                queue.dma_start(out=plane[32 * quad : 32 * quad + 4, :].bitcast(I32),
+                                in_=rows[0, 4 * quad : 4 * quad + 4, :].bitcast(I32))
+
+        c_plane = sb.tile([P, T], U8, align_bytes=64)
+        d_plane = sb.tile([P, U], U8, align_bytes=64)
+        f1 = [sb.tile([P, U], F32, name="f1_%d" % h) for h in range(2)]
+        nc.vector.memset(c_plane[:].bitcast(U32), 0)
+        nc.vector.memset(d_plane[:].bitcast(U32), 0)
+        for window in f1:
+            nc.vector.memset(window[:], 0.0)
+
+        q_raw = sb.tile([P, PACK, Q], F32)
+        nc.sync.dma_start(out=q_raw[:], in_=query.rearrange("(p j) q -> p j q", j=PACK))
+        load_scale_rows(nc.scalar, c_plane, cache_scales)
+        c_flat = cache_words[0].rearrange("p n t -> p (n t)")
+        c_words = []
+        for h in range(2):
+            cw = sb.tile([P, T // 2], U32, align_bytes=64, name="c_words%d" % h, tag="c_words%d" % h)
+            nc.sync.dma_start(out=cw[:].bitcast(I32), in_=c_flat[:, h * 2 * T : (h + 1) * 2 * T].bitcast(I32))
+            c_words.append(cw)
+        sa_col = sb.tile([P, 1], F32)
+        nc.sync.dma_start(out=sa_col[:], in_=sa)
+        l1 = list_tile("l1")
+        nc.sync.dma_start(l1[:], offs)
+        l2 = list_tile("l2")
+        nc.sync.dma_start(l2[:], offs2)
+        d_words = sb.tile([P, 2 * U], U8, align_bytes=64)
+        nc.sync.dma_start(out=d_words[:], in_=draft_words[0])
+        load_scale_rows(nc.sync, d_plane, draft_scales)
+        l4 = list_tile("l4")
+        nc.sync.dma_start(l4[:], offs4)
+        l3 = list_tile("l3")
+        nc.sync.dma_start(l3[:], offs3)
+        l5 = list_tile("l5")
+        nc.sync.dma_start(l5[:], offs5)
+
+        q_grouped = sb.tile([P, Q, PACK], BF16, align_bytes=64, tag="q_grouped")
+        q_halves = [slice(0, Q // 2), slice(Q // 2, Q)]
+        for cols in q_halves:
+            nc.vector.tensor_copy(out=q_grouped[:, cols, :].rearrange("p (c i) t -> p c t i", i=4),
+                                  in_=q_raw[:, :, cols].rearrange("p t (c i) -> p c t i", i=4))
+        q_codes = sb.tile([P, Q], U32, align_bytes=64)
+        q_plane = sb.tile([P, Q], U8, align_bytes=64)
+        for cols in q_halves:
+            nc.vector.quantize_mx(out=q_codes[:, cols].bitcast(FP8X4), scales=q_plane[:, cols],
+                                  in_=q_grouped[:, cols, :].rearrange("p q t -> p (q t)"))
+
+        a = sb.tile([P, T], F32)
+        NA = 256
+        for c in range(T // NA):
+            bank = ps.tile([P, NA], F32, name="a_bank%d" % c)
+            h, lo = divmod(c * NA, T // 2)
+            nc.tensor.matmul_mx(out=bank[:], lhsT=q_codes[:].bitcast(FP8X4), lhsT_scale=q_plane[:],
+                                rhs=c_words[h][:, lo : lo + NA].bitcast(FP8X4),
+                                rhs_scale=c_plane[:, c * NA : (c + 1) * NA], start=True, stop=True)
+            if c % 2 == 0:
+                nc.vector.tensor_copy(out=a[:, c * NA : (c + 1) * NA], in_=bank[:])
+            else:
+                nc.scalar.activation(out=a[:, c * NA : (c + 1) * NA], in_=bank[:], func=COPY)
+
+        f2 = [sb.tile([P, T], F32, align_bytes=64, name="f2_%d" % h, tag=tag)
+              for h, tag in enumerate(["q_grouped", "c_words0"])]
+        for window in f2:
+            nc.gpsimd.memset(window[:], 0.0)
+
+        halves = [(0, HALF), (HALF, I)]
+        w = sb.tile([P, I], F32)
+        v = sb.tile([P, I], F32)
+        for lo, hi in halves:
+            nc.scalar.activation(out=w[:, lo:hi], in_=a[:].indirect(entries(l1, lo, hi)), func=COPY, scale=sa_col[:])
+        for window, (lo, hi) in zip(f1, [(0, 192), (192, I)]):
+            nc.vector.scalar_tensor_tensor(out=v[:, lo:hi], in0=w[:, lo:hi], scalar=0.5, in1=w[:, lo:hi],
+                                           op0=ALU.mult, op1=ALU.mult)
+            nc.scalar.activation(out=window[:].indirect(entries(l2, lo, hi)), in_=v[:, lo:hi], func=COPY)
+
+        b = sb.tile([P, U], F32)
+        NB = 512
+        for c in range(U // NB):
+            bank = ps.tile([P, NB], F32, name="b_bank%d" % c)
+            nc.tensor.matmul_mx(out=bank[:], lhsT=q_codes[:].bitcast(FP8X4), lhsT_scale=q_plane[:],
+                                rhs=d_words[:, 2 * c * NB : 2 * (c + 1) * NB].bitcast(FP4X4),
+                                rhs_scale=d_plane[:, c * NB : (c + 1) * NB], start=True, stop=True)
+            nc.vector.tensor_copy(out=b[:, c * NB : (c + 1) * NB], in_=bank[:])
+
+        bb_part = sb.tile([P, U], F32)
+        nc.vector.tensor_tensor(out=bb_part[:], in0=b[:], in1=f1[0][:], op=ALU.subtract)
+        bb = sb.tile([P, U], F32, tag="bb")
+        nc.vector.tensor_tensor(out=bb[:], in0=bb_part[:], in1=f1[1][:], op=ALU.subtract)
+        bb4 = sb.tile([P, I], F32)
+        nc.vector.tensor_copy(out=bb4[:, 0:HALF], in_=bb[:].indirect(entries(l4, 0, HALF)))
+        nc.scalar.activation(out=bb4[:, HALF:I], in_=bb[:].indirect(entries(l4, HALF, I)), func=COPY)
+        r = sb.tile([P, I], F32)
+        for window, (lo, hi) in zip(f2, [(0, 128), (128, I)]):
+            nc.vector.tensor_tensor(out=r[:, lo:hi], in0=bb4[:, lo:hi], in1=w[:, lo:hi], op=ALU.max)
+            nc.scalar.activation(out=window[:].indirect(entries(l3, lo, hi)), in_=r[:, lo:hi], func=COPY)
+
+        b4 = sb.tile([P, I], F32, tag="bb")
+        nc.vector.tensor_copy(out=b4[:], in_=b[:].indirect(l4[:]))
+        aa_part = sb.tile([P, T], F32)
+        nc.vector.tensor_tensor(out=aa_part[:], in0=a[:], in1=f2[0][:], op=ALU.add)
+        aa = sb.tile([P, T], F32)
+        nc.vector.tensor_tensor(out=aa[:], in0=aa_part[:], in1=f2[1][:], op=ALU.add)
+        aa5 = sb.tile([P, I], F32)
+        nc.vector.tensor_copy(out=aa5[:, 0:HALF], in_=aa[:].indirect(entries(l5, 0, HALF)))
+        nc.scalar.activation(out=aa5[:, HALF:I], in_=aa[:].indirect(entries(l5, HALF, I)), func=COPY)
+        y = sb.tile([P, I], F32)
+        for lo, hi in halves:
+            nc.vector.tensor_tensor(out=y[:, lo:hi], in0=aa5[:, lo:hi], in1=b4[:, lo:hi], op=ALU.min)
+            nc.sync.dma_start(out=out[:, lo:hi], in_=y[:, lo:hi])

@@ -34,22 +34,20 @@ def tile_attend_squaresout_two_kernel(tc, query, cache_words, cache_scales, draf
         def entries(lst, lo, hi):
             return lst[:, lo // 16 : hi // 16]
 
-        def load_scale_rows(queue, plane, rows):
-            for quad in range(4):
+        def load_scale_rows(queues, plane, rows):
+            for quad, queue in enumerate(queues):
                 queue.dma_start(out=plane[32 * quad : 32 * quad + 4, :].bitcast(I32),
                                 in_=rows[0, 4 * quad : 4 * quad + 4, :].bitcast(I32))
 
         c_plane = sb.tile([P, T], U8, align_bytes=64)
         d_plane = sb.tile([P, U], U8, align_bytes=64)
         f1 = [sb.tile([P, U], F32, name="f1_%d" % h) for h in range(2)]
-        nc.vector.memset(c_plane[:].bitcast(U32), 0)
-        nc.vector.memset(d_plane[:].bitcast(U32), 0)
         for window in f1:
             nc.vector.memset(window[:], 0.0)
 
         q_raw = sb.tile([P, PACK, Q], F32)
         nc.sync.dma_start(out=q_raw[:], in_=query.rearrange("(p j) q -> p j q", j=PACK))
-        load_scale_rows(nc.scalar, c_plane, cache_scales)
+        load_scale_rows([nc.sync] * 4, c_plane, cache_scales)
         c_flat = cache_words[0].rearrange("p n t -> p (n t)")
         c_words = []
         for h in range(2):
@@ -60,11 +58,11 @@ def tile_attend_squaresout_two_kernel(tc, query, cache_words, cache_scales, draf
         nc.sync.dma_start(out=sa_col[:], in_=sa)
         l1 = list_tile("l1")
         nc.sync.dma_start(l1[:], offs)
-        l2 = list_tile("l2")
-        nc.sync.dma_start(l2[:], offs2)
         d_words = sb.tile([P, 2 * U], U8, align_bytes=64)
         nc.sync.dma_start(out=d_words[:], in_=draft_words[0])
-        load_scale_rows(nc.sync, d_plane, draft_scales)
+        load_scale_rows([nc.sync] * 4, d_plane, draft_scales)
+        l2 = list_tile("l2")
+        nc.sync.dma_start(l2[:], offs2)
         l4 = list_tile("l4")
         nc.sync.dma_start(l4[:], offs4)
         l3 = list_tile("l3")
@@ -84,17 +82,16 @@ def tile_attend_squaresout_two_kernel(tc, query, cache_words, cache_scales, draf
                                   in_=q_grouped[:, cols, :].rearrange("p q t -> p (q t)"))
 
         a = sb.tile([P, T], F32)
-        NA = 256
-        for c in range(T // NA):
-            bank = ps.tile([P, NA], F32, name="a_bank%d" % c)
-            h, lo = divmod(c * NA, T // 2)
+        for c, (lo, hi) in enumerate([(0, 256), (256, 512), (512, 768), (768, 896), (896, T)]):
+            bank = ps.tile([P, hi - lo], F32, name="a_bank%d" % c)
+            h, first = divmod(lo, T // 2)
             nc.tensor.matmul_mx(out=bank[:], lhsT=q_codes[:].bitcast(FP8X4), lhsT_scale=q_plane[:],
-                                rhs=c_words[h][:, lo : lo + NA].bitcast(FP8X4),
-                                rhs_scale=c_plane[:, c * NA : (c + 1) * NA], start=True, stop=True)
+                                rhs=c_words[h][:, first : first + hi - lo].bitcast(FP8X4),
+                                rhs_scale=c_plane[:, lo:hi], start=True, stop=True)
             if c % 2 == 0:
-                nc.vector.tensor_copy(out=a[:, c * NA : (c + 1) * NA], in_=bank[:])
+                nc.vector.tensor_copy(out=a[:, lo:hi], in_=bank[:])
             else:
-                nc.scalar.activation(out=a[:, c * NA : (c + 1) * NA], in_=bank[:], func=COPY)
+                nc.scalar.activation(out=a[:, lo:hi], in_=bank[:], func=COPY)
 
         f2 = [sb.tile([P, T], F32, align_bytes=64, name="f2_%d" % h, tag=tag)
               for h, tag in enumerate(["q_grouped", "c_words0"])]
@@ -142,6 +139,6 @@ def tile_attend_squaresout_two_kernel(tc, query, cache_words, cache_scales, draf
         nc.vector.tensor_copy(out=aa5[:, 0:HALF], in_=aa[:].indirect(entries(l5, 0, HALF)))
         nc.scalar.activation(out=aa5[:, HALF:I], in_=aa[:].indirect(entries(l5, HALF, I)), func=COPY)
         y = sb.tile([P, I], F32)
-        for lo, hi in halves:
+        for lo, hi in [(0, HALF), (HALF, 384), (384, I)]:
             nc.vector.tensor_tensor(out=y[:, lo:hi], in0=aa5[:, lo:hi], in1=b4[:, lo:hi], op=ALU.min)
             nc.sync.dma_start(out=out[:, lo:hi], in_=y[:, lo:hi])

from contextlib import ExitStack

import concourse.mybir as mybir

D, T, U, I, Q = 512, 1024, 1024, 512, 128
FLOPS = 2 * D * Q * (T + U)

F32 = mybir.dt.float32
BF16 = mybir.dt.bfloat16
I32 = mybir.dt.int32
U32 = mybir.dt.uint32
U16 = mybir.dt.uint16
U8 = mybir.dt.uint8
FP8X4 = mybir.dt.float8_e4m3fn_x4
FP4X4 = mybir.dt.float4_e2m1fn_x4
COPY = mybir.ActivationFunctionType.Copy
ALU = mybir.AluOpType

P = 128
PACK = 4
HALF = I // 2


def tile_attend_squaresout_two_kernel(tc, query, cache_words, cache_scales, draft_words, draft_scales, sa,
                                       offs, offs2, offs3, offs4, offs5, out):
    nc = tc.nc
    with ExitStack() as ctx:
        sb = ctx.enter_context(tc.tile_pool(name="sb", bufs=1))
        ps = ctx.enter_context(tc.psum_pool(name="ps", bufs=1))

        def list_tile(name):
            return sb.tile([P, I // 16], U16, name=name)

        def entries(lst, lo, hi):
            return lst[:, lo // 16 : hi // 16]

        def load_scale_rows(queues, plane, rows):
            for quad, queue in enumerate(queues):
                queue.dma_start(out=plane[32 * quad : 32 * quad + 4, :].bitcast(I32),
                                in_=rows[0, 4 * quad : 4 * quad + 4, :].bitcast(I32))

        c_plane = sb.tile([P, T], U8, align_bytes=64)
        d_plane = sb.tile([P, U], U8, align_bytes=64)
        f1 = [sb.tile([P, U], F32, name="f1_%d" % h) for h in range(2)]
        for window in f1:
            nc.vector.memset(window[:], 0.0)

        q_raw = sb.tile([P, PACK, Q], F32)
        nc.sync.dma_start(out=q_raw[:], in_=query.rearrange("(p j) q -> p j q", j=PACK))
        load_scale_rows([nc.sync] * 4, c_plane, cache_scales)
        c_flat = cache_words[0].rearrange("p n t -> p (n t)")
        c_words = []
        for h in range(2):
            cw = sb.tile([P, T // 2], U32, align_bytes=64, name="c_words%d" % h, tag="c_words%d" % h)
            nc.sync.dma_start(out=cw[:].bitcast(I32), in_=c_flat[:, h * 2 * T : (h + 1) * 2 * T].bitcast(I32))
            c_words.append(cw)
        sa_col = sb.tile([P, 1], F32)
        nc.sync.dma_start(out=sa_col[:], in_=sa)
        l1 = list_tile("l1")
        nc.sync.dma_start(l1[:], offs)
        d_words = sb.tile([P, 2 * U], U8, align_bytes=64)
        nc.sync.dma_start(out=d_words[:], in_=draft_words[0])
        load_scale_rows([nc.sync] * 4, d_plane, draft_scales)
        l2 = list_tile("l2")
        nc.sync.dma_start(l2[:], offs2)
        l4 = list_tile("l4")
        nc.sync.dma_start(l4[:], offs4)
        l3 = list_tile("l3")
        nc.sync.dma_start(l3[:], offs3)
        l5 = list_tile("l5")
        nc.sync.dma_start(l5[:], offs5)

        q_grouped = sb.tile([P, Q, PACK], BF16, align_bytes=64, tag="q_grouped")
        q_halves = [slice(0, Q // 2), slice(Q // 2, Q)]
        for cols in q_halves:
            nc.vector.tensor_copy(out=q_grouped[:, cols, :].rearrange("p (c i) t -> p c t i", i=4),
                                  in_=q_raw[:, :, cols].rearrange("p t (c i) -> p c t i", i=4))
        q_codes = sb.tile([P, Q], U32, align_bytes=64)
        q_plane = sb.tile([P, Q], U8, align_bytes=64)
        for cols in q_halves:
            nc.vector.quantize_mx(out=q_codes[:, cols].bitcast(FP8X4), scales=q_plane[:, cols],
                                  in_=q_grouped[:, cols, :].rearrange("p q t -> p (q t)"))

        a = sb.tile([P, T], F32)
        for c, (lo, hi) in enumerate([(0, 256), (256, 512), (512, 768), (768, 896), (896, T)]):
            bank = ps.tile([P, hi - lo], F32, name="a_bank%d" % c)
            h, first = divmod(lo, T // 2)
            nc.tensor.matmul_mx(out=bank[:], lhsT=q_codes[:].bitcast(FP8X4), lhsT_scale=q_plane[:],
                                rhs=c_words[h][:, first : first + hi - lo].bitcast(FP8X4),
                                rhs_scale=c_plane[:, lo:hi], start=True, stop=True)
            if c % 2 == 0:
                nc.vector.tensor_copy(out=a[:, lo:hi], in_=bank[:])
            else:
                nc.scalar.activation(out=a[:, lo:hi], in_=bank[:], func=COPY)

        f2 = [sb.tile([P, T], F32, align_bytes=64, name="f2_%d" % h, tag=tag)
              for h, tag in enumerate(["q_grouped", "c_words0"])]
        for window in f2:
            nc.gpsimd.memset(window[:], 0.0)

        halves = [(0, HALF), (HALF, I)]
        w = sb.tile([P, I], F32)
        v = sb.tile([P, I], F32)
        for lo, hi in halves:
            nc.scalar.activation(out=w[:, lo:hi], in_=a[:].indirect(entries(l1, lo, hi)), func=COPY, scale=sa_col[:])
        for window, (lo, hi) in zip(f1, [(0, 192), (192, I)]):
            nc.vector.scalar_tensor_tensor(out=v[:, lo:hi], in0=w[:, lo:hi], scalar=0.5, in1=w[:, lo:hi],
                                           op0=ALU.mult, op1=ALU.mult)
            nc.scalar.activation(out=window[:].indirect(entries(l2, lo, hi)), in_=v[:, lo:hi], func=COPY)

        b = sb.tile([P, U], F32)
        NB = 512
        for c in range(U // NB):
            bank = ps.tile([P, NB], F32, name="b_bank%d" % c)
            nc.tensor.matmul_mx(out=bank[:], lhsT=q_codes[:].bitcast(FP8X4), lhsT_scale=q_plane[:],
                                rhs=d_words[:, 2 * c * NB : 2 * (c + 1) * NB].bitcast(FP4X4),
                                rhs_scale=d_plane[:, c * NB : (c + 1) * NB], start=True, stop=True)
            nc.vector.tensor_copy(out=b[:, c * NB : (c + 1) * NB], in_=bank[:])

        bb_part = sb.tile([P, U], F32)
        nc.vector.tensor_tensor(out=bb_part[:], in0=b[:], in1=f1[0][:], op=ALU.subtract)
        bb = sb.tile([P, U], F32, tag="bb")
        nc.vector.tensor_tensor(out=bb[:], in0=bb_part[:], in1=f1[1][:], op=ALU.subtract)
        bb4 = sb.tile([P, I], F32)
        nc.vector.tensor_copy(out=bb4[:, 0:HALF], in_=bb[:].indirect(entries(l4, 0, HALF)))
        nc.scalar.activation(out=bb4[:, HALF:I], in_=bb[:].indirect(entries(l4, HALF, I)), func=COPY)
        r = sb.tile([P, I], F32)
        for window, (lo, hi) in zip(f2, [(0, 128), (128, I)]):
            nc.vector.tensor_tensor(out=r[:, lo:hi], in0=bb4[:, lo:hi], in1=w[:, lo:hi], op=ALU.max)
            nc.scalar.activation(out=window[:].indirect(entries(l3, lo, hi)), in_=r[:, lo:hi], func=COPY)

        b4 = sb.tile([P, I], F32, tag="bb")
        nc.vector.tensor_copy(out=b4[:], in_=b[:].indirect(l4[:]))
        aa_part = sb.tile([P, T], F32)
        nc.vector.tensor_tensor(out=aa_part[:], in0=a[:], in1=f2[0][:], op=ALU.add)
        aa = sb.tile([P, T], F32)
        nc.vector.tensor_tensor(out=aa[:], in0=aa_part[:], in1=f2[1][:], op=ALU.add)
        aa5 = sb.tile([P, I], F32)
        nc.vector.tensor_copy(out=aa5[:, 0:HALF], in_=aa[:].indirect(entries(l5, 0, HALF)))
        nc.scalar.activation(out=aa5[:, HALF:I], in_=aa[:].indirect(entries(l5, HALF, I)), func=COPY)
        y = sb.tile([P, I], F32)
        for lo, hi in [(0, HALF), (HALF, 384), (384, I)]:
            nc.vector.tensor_tensor(out=y[:, lo:hi], in0=aa5[:, lo:hi], in1=b4[:, lo:hi], op=ALU.min)
            nc.sync.dma_start(out=out[:, lo:hi], in_=y[:, lo:hi])
